import numpy as np
import ml_dtypes


def mxq(x, axis, fmt="e4m3"):
    dtype, down = {"e4m3": (ml_dtypes.float8_e4m3fn, 7), "e5m2": (ml_dtypes.float8_e5m2, 14)}[fmt]
    v = np.moveaxis(np.asarray(x, np.float32).astype(ml_dtypes.bfloat16).astype(np.float64), axis, -1)
    blocks = v.reshape(v.shape[:-1] + (-1, 32))
    amax = np.abs(blocks).max(-1, keepdims=True)
    byte = np.maximum(np.where(amax > 0, np.frexp(amax)[1] - 1 + 127, 0) - down, 1)
    scale = np.exp2(byte - 127.0)
    codes = (blocks / scale).astype(np.float32).astype(dtype).astype(np.float64)
    return np.moveaxis((codes * scale).reshape(v.shape), -1, axis)


WIDE = False


def mx_kscale(k):
    if not WIDE:
        return np.ones(k)
    levels = np.array([10, -10, 5, -5, 0])
    if k % 512:
        return np.exp2(np.random.permutation(np.resize(levels, k // 32))).repeat(32)
    a = np.empty((k // 512, 16))
    for p in range(k // 512):
        a[p, :8] = np.random.permutation(np.resize(levels, 8))
        for g in range(8):
            far = levels[np.abs(levels - a[p, g]) >= 10]
            a[p, g + 8] = far[np.random.randint(len(far))]
    return np.exp2(a.ravel()).repeat(32)


def f64(x):
    return np.asarray(x).astype(np.float64)


def striped(idx):
    return np.tile(idx.reshape(-1, 16).T, (8, 1)).astype(np.uint16)


def unstriped(offs):
    return offs[:16].T.reshape(-1).astype(np.int64)


def striped8(idx):
    return np.concatenate([x.reshape(-1, 16).T for x in idx]).astype(np.uint16)


def runs(offs, k):
    lists = np.stack([offs[16 * r : 16 * r + 16].T.reshape(-1) for r in range(8)]).astype(np.int64)
    return lists[np.arange(k) % 512 // 64]


def pack_weight(w):
    k, n = w.shape
    w = f64(np.asarray(w, np.float32).astype(ml_dtypes.bfloat16)).reshape(k // 32, 32, n)
    amax = np.abs(w).max(1)
    byte = np.clip(np.where(amax > 0, np.frexp(amax)[1] - 1 + 127 - 7, 1), 1, 254)
    scaled = (w * np.exp2(127.0 - byte)[:, None, :]).reshape(k, n).astype(np.float32)
    words = np.ascontiguousarray(scaled.reshape(k // 512, 128, 4, n).transpose(0, 1, 3, 2)).astype(ml_dtypes.float8_e4m3fn).view(np.uint8)
    return words, np.ascontiguousarray(byte.astype(np.uint8).reshape(k // 512, 16, n))


def unpack_weight(words, scales):
    g, p, n, _ = words.shape
    vals = np.ascontiguousarray(words).view(ml_dtypes.float8_e4m3fn).astype(np.float64) * np.repeat(np.exp2(scales.astype(np.float64) - 127.0), 8, axis=1)[..., None]
    return vals.transpose(0, 1, 3, 2).reshape(g * 512, n)


E2M1 = np.array([0.0, 0.5, 1.0, 1.5, 2.0, 3.0, 4.0, 6.0, -0.0, -0.5, -1.0, -1.5, -2.0, -3.0, -4.0, -6.0])


def pack_fp4(w):
    k, n = w.shape
    w = f64(np.asarray(w, np.float32).astype(ml_dtypes.bfloat16)).reshape(k // 32, 32, n)
    amax = np.abs(w).max(1)
    mant, ex = np.frexp(amax / 6.0)
    byte = np.clip(np.where(amax > 0, np.where(mant > 0.5, ex, ex - 1) + 127, 1), 1, 254)
    scaled = (w * np.exp2(127.0 - byte)[:, None, :]).reshape(k, n).astype(np.float32)
    c = np.ascontiguousarray(scaled.reshape(k // 512, 128, 4, n).transpose(0, 1, 3, 2)).astype(ml_dtypes.float4_e2m1fn).view(np.uint8) & 0xF
    words = (c[..., 0::2] | (c[..., 1::2] << 4)).reshape(k // 512, 128, 2 * n)
    return np.ascontiguousarray(words), np.ascontiguousarray(byte.astype(np.uint8).reshape(k // 512, 16, n))


def unpack_fp4(words, scales):
    g, _, n = scales.shape
    words = np.ascontiguousarray(words).reshape(g, 128, n, 2)
    nib = np.empty((g, 128, n, 4), np.uint8)
    nib[..., 0::2] = words & 0xF
    nib[..., 1::2] = words >> 4
    vals = E2M1[nib] * np.repeat(np.exp2(scales.astype(np.float64) - 127.0), 8, axis=1)[..., None]
    return vals.transpose(0, 1, 3, 2).reshape(g * 512, n)


def planes(y):
    n, m = y.shape
    v = y.astype(np.float32).astype(ml_dtypes.bfloat16).astype(np.float64).reshape(n // 32, 32, m)
    top = np.abs(v).max(1)
    byte = np.clip(np.where(top > 0, np.frexp(top)[1] - 1 + 127 - 7, 1), 1, 254)
    codes = (v * np.exp2(127.0 - byte)[:, None, :]).reshape(n, m).astype(np.float32).astype(ml_dtypes.float8_e4m3fn).view(np.uint8)
    words = codes.reshape(n // 512, 128, 4, m).transpose(0, 1, 3, 2)
    return np.ascontiguousarray(words), np.ascontiguousarray(byte.astype(np.uint8).reshape(n // 512, 16, m))


K, T, S, V, H = 512, 2048, 512, 512, 512


def setup_inputs():
    n = np.random.standard_normal
    s = mx_kscale(K)[:, None]
    u = mx_kscale(S)
    packed_xT = pack_weight(n((K, T)) * s)
    packed_w1 = pack_fp4(n((K, H)) / np.sqrt(K) / s)
    packed_w2 = pack_fp4(n((K, H)) / np.sqrt(K) / s)
    packed_w3 = pack_fp4(n((K, H)) / np.sqrt(K) / s)
    return {
        "x_words": packed_xT[0],
        "x_scales": packed_xT[1],
        "w1_words": packed_w1[0],
        "w1_scales": packed_w1[1],
        "w2_words": packed_w2[0],
        "w2_scales": packed_w2[1],
        "w3_words": packed_w3[0],
        "w3_scales": packed_w3[1],
        "ga": (np.random.uniform(0.5, 1.5, (H, 1)) * u[:, None]).astype(np.float32),
        "gb": (np.random.uniform(0.5, 1.5, (H, 1)) / u[:, None]).astype(np.float32),
        "offs": striped(np.random.permutation(T)[:S]),
        "two": striped(np.random.permutation(T)[:S]),
        "n1": striped8(np.stack([np.random.permutation(S) for _ in range(8)])),
        "n2": striped8(np.stack([np.random.permutation(S) for _ in range(8)])),
        "three": striped(np.random.permutation(T)[:V]),
        "n3": striped8(np.stack([np.random.permutation(V) for _ in range(8)])),
        "n4": striped8(np.stack([np.random.permutation(V) for _ in range(8)])),
        "n5": striped8(np.stack([np.random.permutation(V) for _ in range(8)])),
        "n6": striped8(np.stack([np.random.permutation(V) for _ in range(8)])),
    }


def reference(x_words, x_scales, w1_words, w1_scales, w2_words, w2_scales, w3_words, w3_scales, ga, gb, offs, two, n1, n2, three, n3, n4, n5, n6):
    xq = unpack_weight(x_words, x_scales)[:, unstriped(offs)]
    y = unpack_fp4(w1_words, w1_scales).T @ xq
    x_two = unpack_weight(x_words, x_scales)[:, unstriped(two)]
    d = unpack_fp4(w2_words, w2_scales).T @ x_two
    z = f64(ga) * (np.maximum(y, d[np.arange(H)[:, None], runs(n2, H)]) - (np.minimum(y[np.arange(H)[:, None], runs(n1, H)], d)))
    x_three = unpack_weight(x_words, x_scales)[:, unstriped(three)]
    b = unpack_fp4(w3_words, w3_scales).T @ x_three
    z2 = f64(gb) * (b[np.arange(H)[:, None], runs(n3, H)] - (b[np.arange(H)[:, None], runs(n4, H)]))
    s = 0.0625 * ((mxq(z, 0, "e4m3").T @ mxq(z2, 0, "e4m3")))
    st = np.maximum(s, s[np.arange(S)[:, None], runs(n5, S)])
    out_0 = np.minimum(st, st[np.arange(S)[:, None], runs(n6, S)])
    return (out_0,) + planes(out_0)

@@ -1,0 +1,285 @@
+from contextlib import ExitStack
+
+import concourse.mybir as mybir
+from concourse.masks import make_identity
+
+FLOPS = 4 * 2 * 512 * 512 * 512
+
+F32 = mybir.dt.float32
+BF16 = mybir.dt.bfloat16
+I32 = mybir.dt.int32
+U32 = mybir.dt.uint32
+U16 = mybir.dt.uint16
+U8 = mybir.dt.uint8
+FP8X4 = mybir.dt.float8_e4m3fn_x4
+FP4X4 = mybir.dt.float4_e2m1fn_x4
+ALU = mybir.AluOpType
+ACT = mybir.ActivationFunctionType
+
+P = 128
+N = 512
+T = 2048
+HALF = 256
+
+
+def tile_picked_twkmaxbgaphopmn_none_po_kernel(
+    tc, x_words, x_scales, w1_words, w1_scales, w2_words, w2_scales, w3_words, w3_scales,
+    ga, gb, offs, two, n1, n2, three, n3, n4, n5, n6, out_0, out_1, out_2,
+):
+    nc = tc.nc
+    with ExitStack() as ctx:
+        keep = ctx.enter_context(tc.tile_pool(name="keep", bufs=1))
+        ring = ctx.enter_context(tc.psum_pool(name="ring", bufs=4))
+        sums = ctx.enter_context(tc.psum_pool(name="sums", bufs=1))
+
+        def sb(shape, dtype, name):
+            return keep.tile(shape, dtype, name=name, align_bytes=64)
+
+        def load_list(src, name):
+            tile = keep.tile([P, N // 16], U16, name=name)
+            nc.sync.dma_start(tile[:], src)
+            return tile
+
+        def load_scale_rows(queue, dst, src):
+            rows = src[0].bitcast(I32)
+            for q in range(4):
+                queue.dma_start(dst[32 * q : 32 * q + 4, :], rows[4 * q : 4 * q + 4, :])
+
+        xs = sb([P, T], U8, "xs")
+        nc.vector.memset(xs[:].bitcast(I32), 0)
+        ws_raw = sb([P, 3 * N // 4], I32, "ws_raw")
+        nc.vector.memset(ws_raw[:], 0)
+
+        offs_t = load_list(offs, "offs_t")
+        load_scale_rows(nc.scalar, xs[:].bitcast(I32), x_scales)
+        two_t = load_list(two, "two_t")
+        three_t = load_list(three, "three_t")
+        xw = sb([P, T], U32, "xw")
+        nc.sync.dma_start(xw[:].bitcast(I32), x_words[0].rearrange("p c r -> p (c r)").bitcast(I32))
+
+        g_rows = sb([P, P], F32, "g_rows")
+        nc.gpsimd.memset(g_rows[:], 0.0)
+        for j, g in enumerate((ga, gb)):
+            nc.gpsimd.dma_start(
+                g_rows[4 * j : 4 * j + 4, :].rearrange("t (g e) -> t g e", e=8),
+                g.rearrange("(g t e) o -> t g (e o)", t=4, e=8),
+            )
+        ident = sb([P, P], F32, "ident")
+        make_identity(nc, ident[:])
+
+        win_a = [sb([P, 2 * N], F32, f"win_a{t}") for t in range(4)]
+        win_b = [sb([P, 2 * N], F32, f"win_b{t}") for t in range(4)]
+        for t in range(4):
+            nc.vector.memset(win_a[t][:, N:], 0.0)
+            nc.vector.memset(win_b[t][:, N:], 0.0)
+
+        ww_raw = []
+        for j, (words, scales) in enumerate(((w1_words, w1_scales), (w2_words, w2_scales), (w3_words, w3_scales))):
+            raw = sb([P, N // 2], I32, f"ww_raw{j}")
+            nc.sync.dma_start(raw[:], words[0].bitcast(I32))
+            load_scale_rows(nc.scalar if j == 0 else nc.sync, ws_raw[:, j * 128 : (j + 1) * 128], scales)
+            ww_raw.append(raw)
+            if j == 1:
+                n2_t = load_list(n2, "n2_t")
+                n1_t = load_list(n1, "n1_t")
+        n4_t = load_list(n4, "n4_t")
+        n3_t = load_list(n3, "n3_t")
+        n5_t = load_list(n5, "n5_t")
+        n6_t = load_list(n6, "n6_t")
+
+        g_bank = ring.tile([P, N], F32, name="bank")
+        nc.tensor.transpose(g_bank[:, :P], g_rows[:], ident[:])
+        g_cols = sb([P, 8], F32, "g_cols")
+        nc.scalar.copy(g_cols[:], g_bank[:, :8])
+        ga_abs = sb([P, 4], F32, "ga_abs")
+        nc.scalar.activation(ga_abs[:], g_cols[:, :4], ACT.Abs)
+        ga_neg = sb([P, 4], F32, "ga_neg")
+        nc.scalar.activation(ga_neg[:], ga_abs[:], ACT.Copy, scale=-1.0)
+
+        xgs = []
+        xgw = []
+        for j, lst in enumerate((offs_t, two_t, three_t)):
+            tile = sb([P, N], U8, f"xgs{j}")
+            nc.vector.tensor_copy(tile[:], xs[:].indirect(lst[:]))
+            xgs.append(tile)
+
+        def deal(j):
+            ww = sb([P, 2 * N], U8, f"ww{j}")
+            nc.vector.tensor_copy(
+                ww[:].bitcast(I32).rearrange("p (t g w) -> p t g w", t=4, w=4),
+                ww_raw[j][:].rearrange("p (g t w) -> p t g w", t=4, w=4),
+            )
+            ws = sb([P, N], U8, f"ws{j}")
+            nc.vector.tensor_copy(
+                ws[:].bitcast(I32).rearrange("p (t g w) -> p t g w", t=4, w=2),
+                ws_raw[:, j * 128 : (j + 1) * 128].rearrange("p (g t w) -> p t g w", t=4, w=2),
+            )
+            return ww, ws
+
+        def gather_words(j, lst):
+            tile = sb([P, N], U32, f"xgw{j}")
+            nc.vector.tensor_copy(tile[:], xw[:].indirect(lst[:]))
+            xgw.append(tile)
+
+        def project(j, w, t, dst, scale):
+            bank = ring.tile([P, N], F32, name="bank")
+            nc.tensor.matmul_mx(
+                out=bank[:],
+                lhsT=w[0][:, 2 * P * t : 2 * P * (t + 1)].bitcast(FP4X4),
+                lhsT_scale=w[1][:, P * t : P * (t + 1)],
+                rhs=xgw[j][:].bitcast(FP8X4),
+                rhs_scale=xgs[j][:],
+                start=True,
+                stop=True,
+            )
+            nc.scalar.activation(dst, bank[:], ACT.Copy, scale=scale[:, t : t + 1])
+
+        w1 = deal(0)
+        gather_words(0, offs_t)
+        w2 = deal(1)
+        gather_words(1, two_t)
+        sign2 = sb([P, 4], F32, "sign2")
+        nc.vector.tensor_scalar(sign2[:], g_cols[:, :4], 0.0, 2.0, ALU.is_ge, ALU.mult)
+        gather_words(2, three_t)
+        gb_signed = sb([P, 4], F32, "gb_signed")
+        nc.vector.scalar_tensor_tensor(gb_signed[:], sign2[:], -1.0, g_cols[:, 4:], ALU.add, ALU.mult)
+        w3 = deal(2)
+
+        for pair in range(2):
+            for t in (2 * pair, 2 * pair + 1):
+                project(0, w1, t, win_a[t][:, :N], ga_abs)
+            for t in (2 * pair, 2 * pair + 1):
+                project(1, w2, t, win_b[t][:, :N], ga_neg)
+        win_q = [sb([P, N], F32, f"win_q{t}") for t in range(4)]
+        for t in range(4):
+            project(2, w3, t, win_q[t][:], gb_signed)
+
+        z_t = [sums.tile([P, N], F32, name=f"z_t{c}") for c in range(4)]
+        for t in range(4):
+            gaps = sb([P, 2 * N], F32, f"gaps{t}")
+            nc.vector.tensor_tensor(gaps[:, :N], win_b[t][:].indirect(n2_t[:]), win_a[t][:, :N], ALU.add)
+            nc.vector.tensor_tensor(gaps[:, N:], win_a[t][:].indirect(n1_t[:]), win_b[t][:, :N], ALU.add)
+            lifts = sb([P, 2 * N], F32, f"lifts{t}")
+            nc.scalar.activation(lifts[:], gaps[:], ACT.Relu, scale=-1.0)
+            for terms, first in (((win_a[t][:, :N], win_b[t][:, :N]), True), ((lifts[:, :N], lifts[:, N:]), False)):
+                for c in range(4):
+                    for j, term in enumerate(terms):
+                        nc.tensor.matmul(
+                            z_t[c][:, P * t : P * (t + 1)],
+                            lhsT=term[:, P * c : P * (c + 1)],
+                            rhs=ident[:],
+                            is_transpose=True,
+                            start=first and j == 0,
+                            stop=(not first) and j == 1,
+                        )
+
+        z_bf = sb([P, 4 * N], BF16, "z_bf")
+        for h in range(2):
+            back = ring.tile([P, N], F32, name="bank")
+            for c in (2 * h, 2 * h + 1):
+                rounded = sb([P, N], BF16, f"rounded{c}")
+                nc.scalar.copy(
+                    rounded[:].rearrange("q (u p e) -> q u p e", u=2, e=2),
+                    z_t[c][:].rearrange("q (u e p) -> q u p e", u=2, e=2),
+                )
+                for u in range(2):
+                    at = HALF * u + P * (c % 2)
+                    nc.tensor.transpose(back[:, at : at + P], rounded[:].bitcast(F32)[:, P * u : P * (u + 1)], ident[:])
+            nc.scalar.copy(
+                z_bf[:].bitcast(F32).rearrange("p (t m u) -> p t m u", t=4, u=2)[:, :, 64 * h : 64 * (h + 1), :],
+                back[:].rearrange("p (u m t) -> p t m u", u=2, t=4),
+            )
+
+        def interleave(engine_copy, dst, src):
+            engine_copy(
+                dst[:].rearrange("p (c i t) -> p c t i", i=4, t=4),
+                src[:].rearrange("p t (c i) -> p c t i", i=4),
+            )
+
+        z2_bf = []
+        for h in range(2):
+            cols = slice(16 * h, 16 * (h + 1))
+            z2 = sb([P, 4, HALF], F32, f"z2_{h}")
+            less = [sb([P, HALF], F32, f"less{h}_{t}") for t in range(4)]
+            for t in range(5):
+                if t < 4:
+                    nc.vector.tensor_copy(less[t][:], win_q[t][:].indirect(n4_t[:, cols]))
+                if t > 0:
+                    nc.vector.tensor_tensor(z2[:, t - 1, :], win_q[t - 1][:].indirect(n3_t[:, cols]), less[t - 1][:], ALU.subtract)
+            bf = sb([P, 4 * HALF], BF16, f"z2_bf{h}")
+            interleave(nc.scalar.copy, bf, z2)
+            z2_bf.append(bf)
+
+        z_w = sb([P, N], U32, "z_w")
+        z_s = sb([P, N], U8, "z_s")
+        nc.vector.quantize_mx(out=z_w[:].bitcast(FP8X4), scales=z_s[:], in_=z_bf[:])
+        z2_w = []
+        z2_s = []
+        for h in range(2):
+            w = sb([P, HALF], U32, f"z2_w{h}")
+            s = sb([P, HALF], U8, f"z2_s{h}")
+            nc.vector.quantize_mx(out=w[:].bitcast(FP8X4), scales=s[:], in_=z2_bf[h][:])
+            z2_w.append(w)
+            z2_s.append(s)
+
+        for t in range(4):
+            bank = ring.tile([P, N], F32, name="bank")
+            for h in range(2):
+                nc.tensor.matmul_mx(
+                    out=bank[:, HALF * h : HALF * (h + 1)],
+                    lhsT=z_w[:, P * t : P * (t + 1)].bitcast(FP8X4),
+                    lhsT_scale=z_s[:, P * t : P * (t + 1)],
+                    rhs=z2_w[h][:].bitcast(FP8X4),
+                    rhs_scale=z2_s[h][:],
+                    start=True,
+                    stop=True,
+                )
+            nc.scalar.activation(win_a[t][:, :N], bank[:], ACT.Copy, scale=0.0625)
+
+        got5 = [sb([P, N], F32, f"got5_{t}") for t in range(4)]
+        got6 = [sb([P, HALF], F32, f"got6_{j}") for j in range(8)]
+        res = [sb([P, 4, HALF], F32, f"res{h}") for h in range(2)]
+        res_bf = [sb([P, 4 * HALF], BF16, f"res_bf{h}") for h in range(2)]
+        o_w = sb([P, N], U32, "o_w")
+        o_s = sb([P, N], U8, "o_s")
+        out_rows = out_0.rearrange("(p t) v -> p t v", t=4)
+        out_words = out_1[0].rearrange("p c r -> p (c r)").bitcast(I32)
+
+        def fetch(step):
+            if step < 4:
+                nc.vector.tensor_copy(got5[step][:], win_a[step][:].indirect(n5_t[:]))
+            else:
+                h, t = divmod(step - 4, 4)
+                nc.vector.tensor_copy(got6[step - 4][:], win_b[t][:].indirect(n6_t[:, 16 * h : 16 * (h + 1)]))
+
+        def combine(step):
+            if step < 4:
+                nc.vector.tensor_tensor(win_b[step][:, :N], win_a[step][:, :N], got5[step][:], ALU.max)
+            else:
+                h, t = divmod(step - 4, 4)
+                cols = slice(HALF * h, HALF * (h + 1))
+                nc.vector.tensor_tensor(res[h][:, t, :], win_b[t][:, cols], got6[step - 4][:], ALU.min)
+                if h == 1:
+                    nc.sync.dma_start(out_rows[:, t, cols], res[h][:, t, :])
+                elif t == 3:
+                    nc.sync.dma_start(out_rows[:, :, cols], res[h][:])
+                    interleave(nc.scalar.copy, res_bf[0], res[0])
+
+        def planes(h):
+            cols = slice(HALF * h, HALF * (h + 1))
+            nc.vector.quantize_mx(out=o_w[:, cols].bitcast(FP8X4), scales=o_s[:, cols], in_=res_bf[h][:])
+            nc.sync.dma_start(out_words[:, cols], o_w[:, cols].bitcast(I32))
+
+        for step in range(13):
+            if step < 12:
+                fetch(step)
+            if step == 12:
+                planes(0)
+            if step > 0:
+                combine(step - 1)
+        interleave(nc.vector.tensor_copy, res_bf[1], res[1])
+        planes(1)
+        out_scales = out_2[0].bitcast(I32)
+        for q in range(4):
+            queue = nc.scalar if q % 2 else nc.sync
+            queue.dma_start(out_scales[4 * q : 4 * q + 4, :], o_s[32 * q : 32 * q + 4, :].bitcast(I32))

@@ -32,8 +32,8 @@ def tile_picked_twkmaxbgaphopmn_none_po_kernel(
         ring = ctx.enter_context(tc.psum_pool(name="ring", bufs=4))
         sums = ctx.enter_context(tc.psum_pool(name="sums", bufs=1))
 
-        def sb(shape, dtype, name):
-            return keep.tile(shape, dtype, name=name, align_bytes=64)
+        def sb(shape, dtype, name, tag=None, bufs=1):
+            return keep.tile(shape, dtype, name=name, tag=tag or name, bufs=bufs, align_bytes=64)
 
         def load_list(src, name):
             tile = keep.tile([P, N // 16], U16, name=name)
@@ -47,45 +47,58 @@ def tile_picked_twkmaxbgaphopmn_none_po_kernel(
 
         xs = sb([P, T], U8, "xs")
         nc.vector.memset(xs[:].bitcast(I32), 0)
-        ws_raw = sb([P, 3 * N // 4], I32, "ws_raw")
-        nc.vector.memset(ws_raw[:], 0)
-
-        offs_t = load_list(offs, "offs_t")
-        load_scale_rows(nc.scalar, xs[:].bitcast(I32), x_scales)
-        two_t = load_list(two, "two_t")
-        three_t = load_list(three, "three_t")
-        xw = sb([P, T], U32, "xw")
-        nc.sync.dma_start(xw[:].bitcast(I32), x_words[0].rearrange("p c r -> p (c r)").bitcast(I32))
-
+        ws_raw = [sb([P, N // 4], I32, f"ws_raw{j}", tag=f"slot_s{j}") for j in range(3)]
+        for j in range(3):
+            nc.vector.memset(ws_raw[j][:], 0)
         g_rows = sb([P, P], F32, "g_rows")
         nc.gpsimd.memset(g_rows[:], 0.0)
-        for j, g in enumerate((ga, gb)):
-            nc.gpsimd.dma_start(
-                g_rows[4 * j : 4 * j + 4, :].rearrange("t (g e) -> t g e", e=8),
-                g.rearrange("(g t e) o -> t g (e o)", t=4, e=8),
-            )
+        zeros = sb([P, N], F32, "zeros")
+        nc.gpsimd.memset(zeros[:], 0.0)
         ident = sb([P, P], F32, "ident")
         make_identity(nc, ident[:])
 
-        win_a = [sb([P, 2 * N], F32, f"win_a{t}") for t in range(4)]
-        win_b = [sb([P, 2 * N], F32, f"win_b{t}") for t in range(4)]
-        for t in range(4):
-            nc.vector.memset(win_a[t][:, N:], 0.0)
-            nc.vector.memset(win_b[t][:, N:], 0.0)
-
-        ww_raw = []
-        for j, (words, scales) in enumerate(((w1_words, w1_scales), (w2_words, w2_scales), (w3_words, w3_scales))):
-            raw = sb([P, N // 2], I32, f"ww_raw{j}")
+        def load_words(j, words):
+            raw = sb([P, N // 2], I32, f"ww_raw{j}", tag=f"slot_w{j}")
             nc.sync.dma_start(raw[:], words[0].bitcast(I32))
-            load_scale_rows(nc.scalar if j == 0 else nc.sync, ws_raw[:, j * 128 : (j + 1) * 128], scales)
-            ww_raw.append(raw)
-            if j == 1:
-                n2_t = load_list(n2, "n2_t")
-                n1_t = load_list(n1, "n1_t")
+            return raw
+
+        def load_gain(j, g):
+            nc.sync.dma_start(
+                g_rows[4 * j : 4 * j + 4, :].rearrange("t (g e) -> t g e", e=8),
+                g.rearrange("(g t e) o -> t g (e o)", t=4, e=8),
+            )
+
+        xs_in = sb([P, T // 4], I32, "xs_in", tag="slot_x")
+        load_scale_rows(nc.sync, xs_in, x_scales)
+        offs_t = load_list(offs, "offs_t")
+        xw = sb([P, T], U32, "xw")
+        nc.sync.dma_start(xw[:].bitcast(I32), x_words[0].rearrange("p c r -> p (c r)").bitcast(I32))
+        two_t = load_list(two, "two_t")
+        three_t = load_list(three, "three_t")
+        load_gain(0, ga)
+        ww_raw = [load_words(0, w1_words)]
+        load_scale_rows(nc.sync, ws_raw[0], w1_scales)
+        load_gain(1, gb)
+        ww_raw.append(load_words(1, w2_words))
+        load_scale_rows(nc.sync, ws_raw[1], w2_scales)
+        n2_t = load_list(n2, "n2_t")
+        n1_t = load_list(n1, "n1_t")
+        ww_raw.append(load_words(2, w3_words))
+        load_scale_rows(nc.sync, ws_raw[2], w3_scales)
         n4_t = load_list(n4, "n4_t")
         n3_t = load_list(n3, "n3_t")
         n5_t = load_list(n5, "n5_t")
         n6_t = load_list(n6, "n6_t")
+
+        win_a = [sb([P, 2 * N], F32, f"win_a{t}") for t in range(4)]
+        win_b = [sb([P, 2 * N], F32, f"win_b{t}") for t in range(4)]
+        for t in range(4):
+            nc.scalar.copy(win_a[t][:, N:], zeros[:])
+            nc.scalar.copy(win_b[t][:, N:], zeros[:])
+
+        for q in range(4):
+            live = slice(32 * q, 32 * q + 4)
+            nc.vector.tensor_copy(xs[:].bitcast(I32)[live, :], xs_in[live, :])
 
         g_bank = ring.tile([P, N], F32, name="bank")
         nc.tensor.transpose(g_bank[:, :P], g_rows[:], ident[:])
@@ -98,26 +111,27 @@ def tile_picked_twkmaxbgaphopmn_none_po_kernel(
 
         xgs = []
         xgw = []
-        for j, lst in enumerate((offs_t, two_t, three_t)):
-            tile = sb([P, N], U8, f"xgs{j}")
+
+        def gather_scales(j, lst, tag):
+            tile = sb([P, N], U8, f"xgs{j}", tag=tag)
             nc.vector.tensor_copy(tile[:], xs[:].indirect(lst[:]))
             xgs.append(tile)
 
         def deal(j):
-            ww = sb([P, 2 * N], U8, f"ww{j}")
+            ws = sb([P, N], U8, f"ws{j}")
+            nc.vector.tensor_copy(
+                ws[:].bitcast(I32).rearrange("p (t g w) -> p t g w", t=4, w=2),
+                ws_raw[j][:].rearrange("p (g t w) -> p t g w", t=4, w=2),
+            )
+            ww = sb([P, 2 * N], U8, f"ww{j}", tag=f"slot_s{j}")
             nc.vector.tensor_copy(
                 ww[:].bitcast(I32).rearrange("p (t g w) -> p t g w", t=4, w=4),
                 ww_raw[j][:].rearrange("p (g t w) -> p t g w", t=4, w=4),
             )
-            ws = sb([P, N], U8, f"ws{j}")
-            nc.vector.tensor_copy(
-                ws[:].bitcast(I32).rearrange("p (t g w) -> p t g w", t=4, w=2),
-                ws_raw[:, j * 128 : (j + 1) * 128].rearrange("p (g t w) -> p t g w", t=4, w=2),
-            )
             return ww, ws
 
-        def gather_words(j, lst):
-            tile = sb([P, N], U32, f"xgw{j}")
+        def gather_words(j, lst, tag):
+            tile = sb([P, N], U32, f"xgw{j}", tag=tag)
             nc.vector.tensor_copy(tile[:], xw[:].indirect(lst[:]))
             xgw.append(tile)
 
@@ -134,16 +148,19 @@ def tile_picked_twkmaxbgaphopmn_none_po_kernel(
             )
             nc.scalar.activation(dst, bank[:], ACT.Copy, scale=scale[:, t : t + 1])
 
+        gather_scales(0, offs_t, None)
+        gather_scales(1, two_t, None)
+        gather_words(0, offs_t, "slot_x")
         w1 = deal(0)
-        gather_words(0, offs_t)
+        gather_words(1, two_t, "slot_w0")
         w2 = deal(1)
-        gather_words(1, two_t)
+        gather_scales(2, three_t, "slot_w1")
         sign2 = sb([P, 4], F32, "sign2")
         nc.vector.tensor_scalar(sign2[:], g_cols[:, :4], 0.0, 2.0, ALU.is_ge, ALU.mult)
-        gather_words(2, three_t)
+        w3 = deal(2)
+        gather_words(2, three_t, "slot_w2")
         gb_signed = sb([P, 4], F32, "gb_signed")
         nc.vector.scalar_tensor_tensor(gb_signed[:], sign2[:], -1.0, g_cols[:, 4:], ALU.add, ALU.mult)
-        w3 = deal(2)
 
         for pair in range(2):
             for t in (2 * pair, 2 * pair + 1):
@@ -177,7 +194,7 @@ def tile_picked_twkmaxbgaphopmn_none_po_kernel(
         for h in range(2):
             back = ring.tile([P, N], F32, name="bank")
             for c in (2 * h, 2 * h + 1):
-                rounded = sb([P, N], BF16, f"rounded{c}")
+                rounded = sb([P, N], BF16, f"rounded{c}", tag=f"slot_r{c}")
                 nc.scalar.copy(
                     rounded[:].rearrange("q (u p e) -> q u p e", u=2, e=2),
                     z_t[c][:].rearrange("q (u e p) -> q u p e", u=2, e=2),
@@ -190,54 +207,67 @@ def tile_picked_twkmaxbgaphopmn_none_po_kernel(
                 back[:].rearrange("p (u m t) -> p t m u", u=2, t=4),
             )
 
-        def interleave(engine_copy, dst, src):
+        def interleave(engine_copy, dst, src, lo, hi):
             engine_copy(
-                dst[:].rearrange("p (c i t) -> p c t i", i=4, t=4),
-                src[:].rearrange("p t (c i) -> p c t i", i=4),
+                dst[:, 4 * lo : 4 * hi].rearrange("p (c i t) -> p c t i", i=4, t=4),
+                src[:, :, lo:hi].rearrange("p t (c i) -> p c t i", i=4),
             )
 
         z2_bf = []
         for h in range(2):
             cols = slice(16 * h, 16 * (h + 1))
-            z2 = sb([P, 4, HALF], F32, f"z2_{h}")
+            z2 = sb([P, 4, HALF], F32, f"z2_{h}", tag=f"slot_z{h}")
             less = [sb([P, HALF], F32, f"less{h}_{t}") for t in range(4)]
             for t in range(5):
                 if t < 4:
                     nc.vector.tensor_copy(less[t][:], win_q[t][:].indirect(n4_t[:, cols]))
                 if t > 0:
                     nc.vector.tensor_tensor(z2[:, t - 1, :], win_q[t - 1][:].indirect(n3_t[:, cols]), less[t - 1][:], ALU.subtract)
-            bf = sb([P, 4 * HALF], BF16, f"z2_bf{h}")
-            interleave(nc.scalar.copy, bf, z2)
+            bf = sb([P, 4 * HALF], BF16, f"z2_bf{h}", tag=("slot_r3", "slot_z0")[h])
+            interleave(nc.scalar.copy, bf, z2, 0, HALF if h == 0 else P)
             z2_bf.append(bf)
 
-        z_w = sb([P, N], U32, "z_w")
-        z_s = sb([P, N], U8, "z_s")
-        nc.vector.quantize_mx(out=z_w[:].bitcast(FP8X4), scales=z_s[:], in_=z_bf[:])
-        z2_w = []
-        z2_s = []
-        for h in range(2):
-            w = sb([P, HALF], U32, f"z2_w{h}")
-            s = sb([P, HALF], U8, f"z2_s{h}")
-            nc.vector.quantize_mx(out=w[:].bitcast(FP8X4), scales=s[:], in_=z2_bf[h][:])
-            z2_w.append(w)
-            z2_s.append(s)
+        z_w = [sb([P, P], U32, f"z_w{t}") for t in range(4)]
+        z_s = [sb([P, P], U8, f"z_s{t}") for t in range(4)]
+        z2_w = [sb([P, HALF], U32, f"z2_w{h}") for h in range(2)]
+        z2_s = [sb([P, HALF], U8, f"z2_s{h}") for h in range(2)]
 
+        def quantize_z(t):
+            nc.vector.quantize_mx(out=z_w[t][:].bitcast(FP8X4), scales=z_s[t][:], in_=z_bf[:, N * t : N * (t + 1)])
+
+        def quantize_z2(h):
+            nc.vector.quantize_mx(out=z2_w[h][:].bitcast(FP8X4), scales=z2_s[h][:], in_=z2_bf[h][:])
+
+        quantize_z(0)
+        quantize_z2(0)
+        interleave(nc.vector.tensor_copy, z2_bf[1], z2, P, HALF)
+        quantize_z(1)
+        quantize_z2(1)
+        quantize_z(2)
+        quantize_z(3)
+
+        s_banks = []
         for t in range(4):
             bank = ring.tile([P, N], F32, name="bank")
+            s_banks.append(bank)
             for h in range(2):
+                cols = slice(HALF * h, HALF * (h + 1))
                 nc.tensor.matmul_mx(
-                    out=bank[:, HALF * h : HALF * (h + 1)],
-                    lhsT=z_w[:, P * t : P * (t + 1)].bitcast(FP8X4),
-                    lhsT_scale=z_s[:, P * t : P * (t + 1)],
+                    out=bank[:, cols],
+                    lhsT=z_w[t][:].bitcast(FP8X4),
+                    lhsT_scale=z_s[t][:],
                     rhs=z2_w[h][:].bitcast(FP8X4),
                     rhs_scale=z2_s[h][:],
                     start=True,
                     stop=True,
                 )
-            nc.scalar.activation(win_a[t][:, :N], bank[:], ACT.Copy, scale=0.0625)
+                if t == 0:
+                    nc.scalar.activation(win_a[t][:, cols], bank[:, cols], ACT.Copy, scale=0.0625)
+            if t > 0:
+                nc.scalar.activation(win_a[t][:, :N], bank[:], ACT.Copy, scale=0.0625)
 
-        got5 = [sb([P, N], F32, f"got5_{t}") for t in range(4)]
-        got6 = [sb([P, HALF], F32, f"got6_{j}") for j in range(8)]
+        got = []
+        win_st = [win_a[(t + 1) % 4] for t in range(4)]
         res = [sb([P, 4, HALF], F32, f"res{h}") for h in range(2)]
         res_bf = [sb([P, 4 * HALF], BF16, f"res_bf{h}") for h in range(2)]
         o_w = sb([P, N], U32, "o_w")
@@ -246,24 +276,27 @@ def tile_picked_twkmaxbgaphopmn_none_po_kernel(
         out_words = out_1[0].rearrange("p c r -> p (c r)").bitcast(I32)
 
         def fetch(step):
+            tile = sb([P, N if step < 4 else HALF], F32, f"got{step}", tag="got", bufs=3)
+            got.append(tile)
             if step < 4:
-                nc.vector.tensor_copy(got5[step][:], win_a[step][:].indirect(n5_t[:]))
+                nc.vector.tensor_copy(tile[:], win_a[step][:].indirect(n5_t[:]))
             else:
                 h, t = divmod(step - 4, 4)
-                nc.vector.tensor_copy(got6[step - 4][:], win_b[t][:].indirect(n6_t[:, 16 * h : 16 * (h + 1)]))
+                nc.vector.tensor_copy(tile[:], win_st[t][:].indirect(n6_t[:, 16 * h : 16 * (h + 1)]))
 
         def combine(step):
+
             if step < 4:
-                nc.vector.tensor_tensor(win_b[step][:, :N], win_a[step][:, :N], got5[step][:], ALU.max)
+                nc.vector.scalar_tensor_tensor(win_st[step][:, :N], s_banks[step][:], 0.0625, got[step][:], ALU.mult, ALU.max)
             else:
                 h, t = divmod(step - 4, 4)
                 cols = slice(HALF * h, HALF * (h + 1))
-                nc.vector.tensor_tensor(res[h][:, t, :], win_b[t][:, cols], got6[step - 4][:], ALU.min)
+                nc.vector.tensor_tensor(res[h][:, t, :], win_st[t][:, cols], got[step][:], ALU.min)
                 if h == 1:
                     nc.sync.dma_start(out_rows[:, t, cols], res[h][:, t, :])
                 elif t == 3:
                     nc.sync.dma_start(out_rows[:, :, cols], res[h][:])
-                    interleave(nc.scalar.copy, res_bf[0], res[0])
+                    interleave(nc.scalar.copy, res_bf[0], res[0], 0, HALF)
 
         def planes(h):
             cols = slice(HALF * h, HALF * (h + 1))
@@ -273,11 +306,11 @@ def tile_picked_twkmaxbgaphopmn_none_po_kernel(
         for step in range(13):
             if step < 12:
                 fetch(step)
-            if step == 12:
-                planes(0)
             if step > 0:
                 combine(step - 1)
-        interleave(nc.vector.tensor_copy, res_bf[1], res[1])
+        interleave(nc.scalar.copy, res_bf[1], res[1], 0, P)
+        planes(0)
+        interleave(nc.vector.tensor_copy, res_bf[1], res[1], P, HALF)
         planes(1)
         out_scales = out_2[0].bitcast(I32)
         for q in range(4):

from contextlib import ExitStack

import concourse.mybir as mybir
from concourse.masks import make_identity

FLOPS = 4 * 2 * 512 * 512 * 512

F32 = mybir.dt.float32
BF16 = mybir.dt.bfloat16
I32 = mybir.dt.int32
U32 = mybir.dt.uint32
U16 = mybir.dt.uint16
U8 = mybir.dt.uint8
FP8X4 = mybir.dt.float8_e4m3fn_x4
FP4X4 = mybir.dt.float4_e2m1fn_x4
ALU = mybir.AluOpType
ACT = mybir.ActivationFunctionType

P = 128
N = 512
T = 2048
HALF = 256


def tile_picked_twkmaxbgaphopmn_none_po_kernel(
    tc, x_words, x_scales, w1_words, w1_scales, w2_words, w2_scales, w3_words, w3_scales,
    ga, gb, offs, two, n1, n2, three, n3, n4, n5, n6, out_0, out_1, out_2,
):
    nc = tc.nc
    with ExitStack() as ctx:
        keep = ctx.enter_context(tc.tile_pool(name="keep", bufs=1))
        ring = ctx.enter_context(tc.psum_pool(name="ring", bufs=4))
        sums = ctx.enter_context(tc.psum_pool(name="sums", bufs=1))

        def sb(shape, dtype, name, tag=None, bufs=1):
            return keep.tile(shape, dtype, name=name, tag=tag or name, bufs=bufs, align_bytes=64)

        def load_list(src, name):
            tile = keep.tile([P, N // 16], U16, name=name)
            nc.sync.dma_start(tile[:], src)
            return tile

        def load_scale_rows(queue, dst, src):
            rows = src[0].bitcast(I32)
            for q in range(4):
                queue.dma_start(dst[32 * q : 32 * q + 4, :], rows[4 * q : 4 * q + 4, :])

        xs = sb([P, T], U8, "xs")
        nc.vector.memset(xs[:].bitcast(I32), 0)
        ws_raw = [sb([P, N // 4], I32, f"ws_raw{j}", tag=f"slot_s{j}") for j in range(3)]
        for j in range(3):
            nc.vector.memset(ws_raw[j][:], 0)
        g_rows = sb([P, P], F32, "g_rows")
        nc.gpsimd.memset(g_rows[:], 0.0)
        zeros = sb([P, N], F32, "zeros")
        nc.gpsimd.memset(zeros[:], 0.0)
        ident = sb([P, P], F32, "ident")
        make_identity(nc, ident[:])

        def load_words(j, words):
            raw = sb([P, N // 2], I32, f"ww_raw{j}", tag=f"slot_w{j}")
            nc.sync.dma_start(raw[:], words[0].bitcast(I32))
            return raw

        def load_gain(j, g):
            nc.sync.dma_start(
                g_rows[4 * j : 4 * j + 4, :].rearrange("t (g e) -> t g e", e=8),
                g.rearrange("(g t e) o -> t g (e o)", t=4, e=8),
            )

        xs_in = sb([P, T // 4], I32, "xs_in", tag="slot_x")
        load_scale_rows(nc.sync, xs_in, x_scales)
        offs_t = load_list(offs, "offs_t")
        xw = sb([P, T], U32, "xw")
        nc.sync.dma_start(xw[:].bitcast(I32), x_words[0].rearrange("p c r -> p (c r)").bitcast(I32))
        two_t = load_list(two, "two_t")
        three_t = load_list(three, "three_t")
        load_gain(0, ga)
        ww_raw = [load_words(0, w1_words)]
        load_scale_rows(nc.sync, ws_raw[0], w1_scales)
        load_gain(1, gb)
        ww_raw.append(load_words(1, w2_words))
        load_scale_rows(nc.sync, ws_raw[1], w2_scales)
        n2_t = load_list(n2, "n2_t")
        n1_t = load_list(n1, "n1_t")
        ww_raw.append(load_words(2, w3_words))
        load_scale_rows(nc.sync, ws_raw[2], w3_scales)
        n4_t = load_list(n4, "n4_t")
        n3_t = load_list(n3, "n3_t")
        n5_t = load_list(n5, "n5_t")
        n6_t = load_list(n6, "n6_t")

        win_a = [sb([P, 2 * N], F32, f"win_a{t}") for t in range(4)]
        win_b = [sb([P, 2 * N], F32, f"win_b{t}") for t in range(4)]
        for t in range(4):
            nc.scalar.copy(win_a[t][:, N:], zeros[:])
            nc.scalar.copy(win_b[t][:, N:], zeros[:])

        for q in range(4):
            live = slice(32 * q, 32 * q + 4)
            nc.vector.tensor_copy(xs[:].bitcast(I32)[live, :], xs_in[live, :])

        g_bank = ring.tile([P, N], F32, name="bank")
        nc.tensor.transpose(g_bank[:, :P], g_rows[:], ident[:])
        g_cols = sb([P, 8], F32, "g_cols")
        nc.scalar.copy(g_cols[:], g_bank[:, :8])
        ga_abs = sb([P, 4], F32, "ga_abs")
        nc.scalar.activation(ga_abs[:], g_cols[:, :4], ACT.Abs)
        ga_neg = sb([P, 4], F32, "ga_neg")
        nc.scalar.activation(ga_neg[:], ga_abs[:], ACT.Copy, scale=-1.0)

        xgs = []
        xgw = []

        def gather_scales(j, lst, tag):
            tile = sb([P, N], U8, f"xgs{j}", tag=tag)
            nc.vector.tensor_copy(tile[:], xs[:].indirect(lst[:]))
            xgs.append(tile)

        def deal(j):
            ws = sb([P, N], U8, f"ws{j}")
            nc.vector.tensor_copy(
                ws[:].bitcast(I32).rearrange("p (t g w) -> p t g w", t=4, w=2),
                ws_raw[j][:].rearrange("p (g t w) -> p t g w", t=4, w=2),
            )
            ww = sb([P, 2 * N], U8, f"ww{j}", tag=f"slot_s{j}")
            nc.vector.tensor_copy(
                ww[:].bitcast(I32).rearrange("p (t g w) -> p t g w", t=4, w=4),
                ww_raw[j][:].rearrange("p (g t w) -> p t g w", t=4, w=4),
            )
            return ww, ws

        def gather_words(j, lst, tag):
            tile = sb([P, N], U32, f"xgw{j}", tag=tag)
            nc.vector.tensor_copy(tile[:], xw[:].indirect(lst[:]))
            xgw.append(tile)

        def project(j, w, t, dst, scale):
            bank = ring.tile([P, N], F32, name="bank")
            nc.tensor.matmul_mx(
                out=bank[:],
                lhsT=w[0][:, 2 * P * t : 2 * P * (t + 1)].bitcast(FP4X4),
                lhsT_scale=w[1][:, P * t : P * (t + 1)],
                rhs=xgw[j][:].bitcast(FP8X4),
                rhs_scale=xgs[j][:],
                start=True,
                stop=True,
            )
            nc.scalar.activation(dst, bank[:], ACT.Copy, scale=scale[:, t : t + 1])

        gather_scales(0, offs_t, None)
        gather_scales(1, two_t, None)
        gather_words(0, offs_t, "slot_x")
        w1 = deal(0)
        gather_words(1, two_t, "slot_w0")
        w2 = deal(1)
        gather_scales(2, three_t, "slot_w1")
        sign2 = sb([P, 4], F32, "sign2")
        nc.vector.tensor_scalar(sign2[:], g_cols[:, :4], 0.0, 2.0, ALU.is_ge, ALU.mult)
        w3 = deal(2)
        gather_words(2, three_t, "slot_w2")
        gb_signed = sb([P, 4], F32, "gb_signed")
        nc.vector.scalar_tensor_tensor(gb_signed[:], sign2[:], -1.0, g_cols[:, 4:], ALU.add, ALU.mult)

        for pair in range(2):
            for t in (2 * pair, 2 * pair + 1):
                project(0, w1, t, win_a[t][:, :N], ga_abs)
            for t in (2 * pair, 2 * pair + 1):
                project(1, w2, t, win_b[t][:, :N], ga_neg)
        win_q = [sb([P, N], F32, f"win_q{t}") for t in range(4)]
        for t in range(4):
            project(2, w3, t, win_q[t][:], gb_signed)

        z_t = [sums.tile([P, N], F32, name=f"z_t{c}") for c in range(4)]
        for t in range(4):
            gaps = sb([P, 2 * N], F32, f"gaps{t}")
            nc.vector.tensor_tensor(gaps[:, :N], win_b[t][:].indirect(n2_t[:]), win_a[t][:, :N], ALU.add)
            nc.vector.tensor_tensor(gaps[:, N:], win_a[t][:].indirect(n1_t[:]), win_b[t][:, :N], ALU.add)
            lifts = sb([P, 2 * N], F32, f"lifts{t}")
            nc.scalar.activation(lifts[:], gaps[:], ACT.Relu, scale=-1.0)
            for terms, first in (((win_a[t][:, :N], win_b[t][:, :N]), True), ((lifts[:, :N], lifts[:, N:]), False)):
                for c in range(4):
                    for j, term in enumerate(terms):
                        nc.tensor.matmul(
                            z_t[c][:, P * t : P * (t + 1)],
                            lhsT=term[:, P * c : P * (c + 1)],
                            rhs=ident[:],
                            is_transpose=True,
                            start=first and j == 0,
                            stop=(not first) and j == 1,
                        )

        z_bf = sb([P, 4 * N], BF16, "z_bf")
        for h in range(2):
            back = ring.tile([P, N], F32, name="bank")
            for c in (2 * h, 2 * h + 1):
                rounded = sb([P, N], BF16, f"rounded{c}", tag=f"slot_r{c}")
                nc.scalar.copy(
                    rounded[:].rearrange("q (u p e) -> q u p e", u=2, e=2),
                    z_t[c][:].rearrange("q (u e p) -> q u p e", u=2, e=2),
                )
                for u in range(2):
                    at = HALF * u + P * (c % 2)
                    nc.tensor.transpose(back[:, at : at + P], rounded[:].bitcast(F32)[:, P * u : P * (u + 1)], ident[:])
            nc.scalar.copy(
                z_bf[:].bitcast(F32).rearrange("p (t m u) -> p t m u", t=4, u=2)[:, :, 64 * h : 64 * (h + 1), :],
                back[:].rearrange("p (u m t) -> p t m u", u=2, t=4),
            )

        def interleave(engine_copy, dst, src, lo, hi):
            engine_copy(
                dst[:, 4 * lo : 4 * hi].rearrange("p (c i t) -> p c t i", i=4, t=4),
                src[:, :, lo:hi].rearrange("p t (c i) -> p c t i", i=4),
            )

        z2_bf = []
        for h in range(2):
            cols = slice(16 * h, 16 * (h + 1))
            z2 = sb([P, 4, HALF], F32, f"z2_{h}", tag=f"slot_z{h}")
            less = [sb([P, HALF], F32, f"less{h}_{t}") for t in range(4)]
            for t in range(5):
                if t < 4:
                    nc.vector.tensor_copy(less[t][:], win_q[t][:].indirect(n4_t[:, cols]))
                if t > 0:
                    nc.vector.tensor_tensor(z2[:, t - 1, :], win_q[t - 1][:].indirect(n3_t[:, cols]), less[t - 1][:], ALU.subtract)
            bf = sb([P, 4 * HALF], BF16, f"z2_bf{h}", tag=("slot_r3", "slot_z0")[h])
            interleave(nc.scalar.copy, bf, z2, 0, HALF if h == 0 else P)
            z2_bf.append(bf)

        z_w = [sb([P, P], U32, f"z_w{t}") for t in range(4)]
        z_s = [sb([P, P], U8, f"z_s{t}") for t in range(4)]
        z2_w = [sb([P, HALF], U32, f"z2_w{h}") for h in range(2)]
        z2_s = [sb([P, HALF], U8, f"z2_s{h}") for h in range(2)]

        def quantize_z(t):
            nc.vector.quantize_mx(out=z_w[t][:].bitcast(FP8X4), scales=z_s[t][:], in_=z_bf[:, N * t : N * (t + 1)])

        def quantize_z2(h):
            nc.vector.quantize_mx(out=z2_w[h][:].bitcast(FP8X4), scales=z2_s[h][:], in_=z2_bf[h][:])

        quantize_z(0)
        quantize_z2(0)
        interleave(nc.vector.tensor_copy, z2_bf[1], z2, P, HALF)
        quantize_z(1)
        quantize_z2(1)
        quantize_z(2)
        quantize_z(3)

        s_banks = []
        for t in range(4):
            bank = ring.tile([P, N], F32, name="bank")
            s_banks.append(bank)
            for h in range(2):
                cols = slice(HALF * h, HALF * (h + 1))
                nc.tensor.matmul_mx(
                    out=bank[:, cols],
                    lhsT=z_w[t][:].bitcast(FP8X4),
                    lhsT_scale=z_s[t][:],
                    rhs=z2_w[h][:].bitcast(FP8X4),
                    rhs_scale=z2_s[h][:],
                    start=True,
                    stop=True,
                )
                if t == 0:
                    nc.scalar.activation(win_a[t][:, cols], bank[:, cols], ACT.Copy, scale=0.0625)
            if t > 0:
                nc.scalar.activation(win_a[t][:, :N], bank[:], ACT.Copy, scale=0.0625)

        got = []
        win_st = [win_a[(t + 1) % 4] for t in range(4)]
        res = [sb([P, 4, HALF], F32, f"res{h}") for h in range(2)]
        res_bf = [sb([P, 4 * HALF], BF16, f"res_bf{h}") for h in range(2)]
        o_w = sb([P, N], U32, "o_w")
        o_s = sb([P, N], U8, "o_s")
        out_rows = out_0.rearrange("(p t) v -> p t v", t=4)
        out_words = out_1[0].rearrange("p c r -> p (c r)").bitcast(I32)

        def fetch(step):
            tile = sb([P, N if step < 4 else HALF], F32, f"got{step}", tag="got", bufs=3)
            got.append(tile)
            if step < 4:
                nc.vector.tensor_copy(tile[:], win_a[step][:].indirect(n5_t[:]))
            else:
                h, t = divmod(step - 4, 4)
                nc.vector.tensor_copy(tile[:], win_st[t][:].indirect(n6_t[:, 16 * h : 16 * (h + 1)]))

        def combine(step):

            if step < 4:
                nc.vector.scalar_tensor_tensor(win_st[step][:, :N], s_banks[step][:], 0.0625, got[step][:], ALU.mult, ALU.max)
            else:
                h, t = divmod(step - 4, 4)
                cols = slice(HALF * h, HALF * (h + 1))
                nc.vector.tensor_tensor(res[h][:, t, :], win_st[t][:, cols], got[step][:], ALU.min)
                if h == 1:
                    nc.sync.dma_start(out_rows[:, t, cols], res[h][:, t, :])
                elif t == 3:
                    nc.sync.dma_start(out_rows[:, :, cols], res[h][:])
                    interleave(nc.scalar.copy, res_bf[0], res[0], 0, HALF)

        def planes(h):
            cols = slice(HALF * h, HALF * (h + 1))
            nc.vector.quantize_mx(out=o_w[:, cols].bitcast(FP8X4), scales=o_s[:, cols], in_=res_bf[h][:])
            nc.sync.dma_start(out_words[:, cols], o_w[:, cols].bitcast(I32))

        for step in range(13):
            if step < 12:
                fetch(step)
            if step > 0:
                combine(step - 1)
        interleave(nc.scalar.copy, res_bf[1], res[1], 0, P)
        planes(0)
        interleave(nc.vector.tensor_copy, res_bf[1], res[1], P, HALF)
        planes(1)
        out_scales = out_2[0].bitcast(I32)
        for q in range(4):
            queue = nc.scalar if q % 2 else nc.sync
            queue.dma_start(out_scales[4 * q : 4 * q + 4, :], o_s[32 * q : 32 * q + 4, :].bitcast(I32))
